import numpy as np, ml_dtypes
CORES = [1,5,17,21,33,37,49,53]
N = 8
import mx_ref
BF = ml_dtypes.bfloat16
def gcols(t, e):
    v = np.concatenate([t.reshape(8, 16, -1, 4), np.zeros((8, 16, 1, 4), BF)], axis=2)
    return np.ascontiguousarray(np.stack([v[g][:, e[g]] for g in range(8)])).reshape(128, -1)
def tile(rs):
    return np.stack(rs, axis=2).reshape(128, -1).astype(BF)
def pick(q, e):
    c = np.concatenate([q[0].reshape(128, -1, 4), np.zeros((128, 1, 4), np.uint8)], axis=1); s = np.concatenate([q[1], np.ones((16, 1), np.uint8)], axis=1)
    return (np.ascontiguousarray(c[:, e].reshape(128, -1)), np.ascontiguousarray(s[:, e]))
def join(*qs):
    return (np.concatenate([q[0] for q in qs], axis=1), np.concatenate([q[1] for q in qs], axis=1))
def put(q, e, v):
    c, s = q[0].reshape(128, -1, 4).copy(), q[1].copy(); c[:, e] = v[0].reshape(128, -1, 4); s[:, e] = v[1]
    return (c.reshape(128, -1), s)
def pk(c, s):
    return (np.ascontiguousarray(c), mx_ref.live(s))
def emit(q):
    return q[0], q[1]
def packed(v, rng):
    q = [mx_ref.quantize(np.ascontiguousarray(v[r])) for r in range(N)]
    return np.stack([a for a, b in q]), np.stack([mx_ref.plane(b, rng) for a, b in q])
def values_of_codes():
    e, c = np.zeros((128, 128, 4), np.float32), np.zeros((128, 2, 4), np.uint8)
    e[np.arange(128), np.arange(128), 0] = 1
    c[:127, :, 0] = np.arange(256).reshape(2, 128).T[:127]
    return mx_ref.matmul(mx_ref.quantize(e.reshape(128, 512).astype(BF)), (c.reshape(128, 8), np.full((16, 2), 127, np.uint8))).T.reshape(-1).astype(np.float64)
CODE_VALUE, SCALE_VALUE = values_of_codes(), 2.0 ** (np.arange(256) - 127.0)
def decode(q):
    return (CODE_VALUE[q[0]].reshape(16, 8, -1, 4) * SCALE_VALUE[q[1]][:, None, :, None] + 0.0).reshape(128, -1).astype(np.float32)
def f(rng, *shape):
    return mx_ref.flush((rng.standard_normal(shape, dtype=np.float32) * np.exp2(rng.integers(-2, 3, shape[:-1] + (1,)))).astype(BF))
def wide(rng, *shape, cols=0):
    v = rng.standard_normal(shape, dtype=np.float32) * np.exp2(rng.integers(-12, 13, shape)).astype(np.float32)
    if cols: v *= np.repeat(np.exp2(rng.integers(-cols, cols + 1, shape[:-2] + (1, shape[-1] // 4))) * (rng.random(shape[:-2] + (1, shape[-1] // 4)) > 0.0625), 4, axis=-1).astype(np.float32)
    return mx_ref.flush(v.astype(BF))
C, M, R = 160, 64, 3
HALF = np.arange(C) // 2
def order(p):
    return np.argsort(-(p + np.float32(0.0)), axis=1, kind="stable")
def gput(t, e, h):
    a, b = t.reshape(8, 16, -1, 4).copy(), h.reshape(8, 16, -1, 4)
    for g in range(8): a[g][:, e[g]] = b[g]
    return a.reshape(128, -1)
def trials(q, t, o):
    s = []
    for g in range(0, 8, 2):
        e = np.concatenate([np.where(np.arange(8)[:, None] == k, o, o[:, HALF]) for k in (g, g + 1)], axis=1)
        p = mx_ref.matmul(q, mx_ref.quantize(gcols(t, e)))
        s += [p[16 * g, :C], p[16 * g + 16, C:]]
    return np.stack(s)
def big(v):
    v = v.astype(np.float32)
    v[np.abs(v) < np.float32(2.0 ** -16)] = 0
    return v.astype(BF)
def numbers_of(rng):
    return {"x": big(f(rng, N, 128, 4 * C)), "u": np.array(f(rng, N, 128, 512)), "v": np.array(f(rng, N, 128, 512))}
def layers(rng):
    return big(f(rng, N, 128, 2048)).reshape(N, 8, 16, 4, 8, 16, 4)
def weights(rng, w):
    c, p = packed(np.ascontiguousarray(w).reshape(N, 128, 2048), rng)
    return {"wc": c, "ws": p}
def signs(rng):
    return np.stack([rng.permutation(8) % 2 * 2.0 - 1.0 for r in range(N)])
def setup_inputs(rng):
    return {**numbers_of(rng), **weights(rng, layers(rng))}
def setup_inputs_ties(rng):
    d = numbers_of(rng)
    e = rng.permutation(N)
    x = d["x"].reshape(N, 8, 16, C, 4)
    u = d["u"].reshape(N, 8, 16, 128, 4)
    u[:, :, 8:, ::16] = 0
    for r in range(N):
        k = np.zeros(C, int) if r == e[0] else rng.permutation(C) % 3
        a = x[r][:, :8, :3].copy()
        a[:, :, 2] = 0
        x[r][:, :8] = a[:, :, k]
        for g in rng.permutation(8)[:4]: u[r, g, :, 16 * g] = 0
    x[e[1]] = 0
    w = layers(rng)
    w[:, :, :, :, :, :8] = 0
    return {"x": x.reshape(N, 128, 4 * C), "u": u.reshape(N, 128, 512), "v": d["v"], **weights(rng, w)}
def setup_inputs_near(rng):
    d = numbers_of(rng)
    x = d["x"].astype(np.float32).reshape(N, 8, 16, C, 4)
    u = d["u"].reshape(N, 128, 128, 4)
    u[:, :, ::16] = 0
    o, c, j = rng.permutation(N) % 4, signs(rng), np.arange(C)
    upper = j // (C // 2)
    own = np.arange(128)[:, None, None] // 16 == np.arange(8)[:, None]
    for r in range(N):
        if o[r] == 3:
            k = rng.choice([-1.0, 1.0], (128, 8, 4)) * rng.integers(8, 16, (128, 8, 4)) * 0.125
            u[r, :, ::16] = (k * np.where(own, 2.0 ** -18, 1.0)).astype(np.float32).astype(BF)
            continue
        a = rng.integers(0, C, (8, 1))
        s = (j + a) % (C // 2) if o[r] == 2 else (j + a) % C // 2
        size = 2.0 ** -4 if o[r] == 2 else 1.0
        z = ((s[:, :, None] >> np.arange(8)) & 1) * np.exp2(np.arange(8) - 23.0) * size
        x[r] = 0
        if o[r] == 2:
            x[r, :, 0, :, 0] = np.where(c[r][:, None] > 0, (8 + upper) * 2.0 ** -30, 9 * upper * 2.0 ** -33)
            x[r, :, 1, :, 0] = np.where(c[r][:, None] > 0, 0.0, 10 * (1 - upper) * 2.0 ** -33)
        else:
            x[r, :, 0, :, 0] = c[r][:, None]
            for i in rng.permutation(8)[:4]: x[r, i, 0, rng.integers(C), 0] *= np.float32(2.0 ** 30)
        x[r, :, 8] = z[:, :, :4]
        x[r, :, 9] = z[:, :, 4:]
        x[r, :, 10:] = rng.integers(4, 8, (8, 6, C, 4)) * 2.0 ** -20 * size
        k = 1.0 if o[r] == 0 else 2.0 ** -30
        for h in range(0, 128, 16):
            u[r, h, h, 0] = k
            u[r, h + 8:h + 10, h] = k
            if o[r] == 2 and c[r, h // 16] < 0:
                u[r, h, h, 0] = 9 * 2.0 ** -33
                u[r, h + 1, h, 0] = 2.0 ** -30
    w = layers(rng)
    w[:, :, :10] = 0
    w[:, :, :, :, :, :10] = 0
    return {"x": x.reshape(N, 128, 4 * C).astype(BF), "u": u.reshape(N, 128, 512), "v": d["v"], **weights(rng, w)}
def setup_inputs_huge(rng):
    d = numbers_of(rng)
    c = np.stack([rng.permutation(C) % 2 * 2.0 - 1.0 for r in range(N)])
    c[rng.permutation(N) < N // 2] = -1
    x = (0.6 + 0.2 * rng.random((N, 128, C, 4))) * np.where(c < 0, -2.0 ** 30, 2.0 ** 28)[:, None, :, None]
    u = d["u"].reshape(N, 128, 128, 4)
    s = signs(rng)
    a = 2.0 ** 30 * (1 - 0.25 * rng.random((N, 128, 8, 4))) * s[:, None, :, None]
    for r in range(N):
        if (c[r] < 0).all():
            x[r, :, rng.integers(C)] = -2.0 ** 30
            a[r, :, rng.choice(np.flatnonzero(s[r] > 0))] = 2.0 ** 30
    u[:, :, ::16] = a.astype(np.float32).astype(BF)
    w = np.zeros((N, 128, 4, 128, 4), np.float32)
    i = np.arange(128)
    for b in range(4): w[:, i, b, i, b] = 16
    return {"x": x.astype(np.float32).reshape(N, 128, 4 * C).astype(BF), "u": u.reshape(N, 128, 512), "v": d["v"], **weights(rng, w.astype(BF))}
def setup_inputs_twice(rng):
    d = numbers_of(rng)
    e = 2 + np.arange(32).reshape(8, 4) // 2
    n = (N, 16, 8, C, 4)
    x = rng.choice([-1.0, 1.0], n) * (9 + 2 * rng.integers(0, 4, n)) * 0.125 * np.exp2(0.0 - e)[:, None]
    x[:, :, 0] = 0
    x[:, :, 0, :, 0] = 1.96875 * rng.choice([-1.0, 1.0], (N, 16, C))
    x *= np.exp2(rng.integers(1, 5, (N, 16, 1, C, 1)))
    u = d["u"].reshape(N, 16, 8, 128, 4)
    k = rng.choice([-1.0, 1.0], (N, 16, 8, 8, 4)) * rng.integers(8, 16, (N, 16, 8, 8, 4)) * 0.125 * np.exp2(e - 17.0)[:, None]
    k[:, :, 0] = 0
    u[:, :, :, ::16] = k.astype(np.float32).astype(BF)
    return {"x": x.astype(np.float32).reshape(N, 128, 4 * C).astype(BF), "u": u.reshape(N, 128, 512), "v": d["v"], **weights(rng, layers(rng))}
def setup_inputs_spread(rng):
    d = setup_inputs(rng)
    d["x"] = big(wide(rng, N, 128, 4 * C, cols=6))
    return d
def check_inputs(d):
    b = []
    for k in ("x", "u", "v"):
        a = np.abs(d[k].astype(np.float32))
        if not (np.isfinite(a).all() and ((a == 0) | (a >= 2.0 ** -30) & (a <= 2.0 ** 30)).all()): b.append("a value of " + k)
    none, least, most = [emit(mx_ref.quantize(np.full((128, 16), k, np.float32).astype(BF)))[1][0, 0] for k in (0.0, 2.0 ** -30, 2.0 ** 30)]
    for r in range(N):
        if ((d["wc"][r] == 0x7F) | (d["wc"][r] == 0xFF)).any(): b.append("wc: a code that is no number")
        s = mx_ref.live(d["ws"][r])
        if ((s != none) & ((s < least) | (s > most))).any(): b.append("ws: a scale out of range")
    return b
def reference(x, u, v, wc, ws):
    qu = [mx_ref.quantize(u[r]) for r in range(N)]
    lay = [pk(wc[r], ws[r]) for r in range(N)]
    now = [x[r] for r in range(N)]
    o = [order(mx_ref.matmul(qu[r], mx_ref.quantize(x[r]))[::16]) for r in range(N)]
    for t in range(R):
        sent = []
        for r in range(N):
            now[r] = decode(mx_ref.quantize(now[r])).astype(BF)
            score = np.zeros((8, C), np.float32)
            np.put_along_axis(score, o[r], trials(qu[r], now[r], o[r]), axis=1)
            o[r] = order(score)
            sent.append(mx_ref.quantize(gcols(now[r], o[r][:, :M])))
        for r in range(N):
            q = sent[(r - 1 - t) % N]
            c = decode(q)
            h = tile([np.maximum(mx_ref.matmul(pick(lay[r], np.arange(128 * b, 128 * b + 128)), q), np.float32(0.0)) * np.float32(0.03125) + c[:, b::4] for b in range(4)])
            now[r] = gput(now[r], o[r][:, C - M:], h)
    y, ol = np.zeros((N, 128, C), np.float32), np.zeros((N, 8, C), np.float32)
    oc, osc = np.zeros((N, 128, 4 * C), np.uint8), np.zeros((N, 16, C), np.uint8)
    for r in range(N):
        q = mx_ref.quantize(now[r])
        y[r] = mx_ref.matmul(mx_ref.quantize(v[r]), q)
        ol[r] = o[r]
        oc[r], osc[r] = emit(q)
    return {"y": y, "ol": ol, "oc": oc, "osc": osc}

@@ -1,0 +1,486 @@
+from concourse.mybir import dt, AluOpType, ActivationFunctionType
+
+ALU = AluOpType
+ACT = ActivationFunctionType
+C, M, R, KEEP = 160, 64, 3, 96
+PL_W = C + M
+BF, F32, I32, U16, QX, U8 = "bfloat16", "float32", "int32", "uint16", "float8_e4m3fn_x4", "uint8"
+
+
+def _scratch():
+    s = {}
+
+    def b(name, n, d, where="sbuf"):
+        s[name] = (where, [128, n], d)
+
+    def q(name, n):
+        b("q" + name, n, QX)
+        b("s" + name, n, U8)
+    for name, n in (("xt", 640), ("ut", 512), ("vt", 512), ("et", 516), ("ones", 516), ("t0", 640), ("si", 640),
+                    ("sp", 4 * PL_W), ("ke", 512), ("kl", 512), ("abe", 768), ("abl", 512), ("gp", 640), ("bt", 512),
+                    ("tf", 640), ("cm", 1600), ("db", 160), ("dc", 160), ("rst", 160),
+                    ("ir", 160), ("val0", 160), ("val1", 160), ("inv", 192), ("tt", 352)):
+        b("b_" + name, n, BF)
+    for name, n in (("pc", 32), ("c40", 40), ("q16", 160), ("lt", 180), ("xs", 320), ("row", 192), ("xtt", 352),
+                    ("col", 16), ("ncol", 16), ("acc", 10), ("rk0", 10), ("rk1", 10), ("rl", 256), ("olr", 160),
+                    ("yo", 160), ("f1", 10), ("f2", 10), ("f3", 10), ("f4", 10)):
+        b("b_" + name, n, F32)
+    b("b_pi", 8, I32)
+    b("b_up", 8, I32)
+    for name, n in (("lu", 180), ("ru", 10), ("rs", 10), ("fl", 10), ("ls3", 16)):
+        b("b_" + name, n, U16)
+    for t in range(R):
+        b("b_ls%d" % t, 16, U16)
+        b("b_ll%d" % t, 4, U16)
+        q("g%d" % t, C)
+    for t in (1, 2):
+        q("se%d" % t, 128)
+        q("sl%d" % t, 128)
+    for name, n in (("x", C), ("u", 128), ("up", 128), ("v", 128), ("w", 512), ("e", 512), ("ab", 448), ("ye", 768),
+                    ("yl", 512), ("b", 192), ("f", C)):
+        q(name, n)
+    b("pa", 2048, F32, "psum")
+    b("pb", 2048, F32, "psum")
+    return s
+
+
+SCRATCH = _scratch()
+DMAS = ["dx", "du", "dv", "dwc", "dws", "dol", "doc", "ds0", "ds1", "ds2", "ds3", "dy"]
+SEMAPHORES = ["nv", "na", "np_", "ng", "sent"] + DMAS + ["ag%d" % t for t in range(R)] + ["al%d" % t for t in range(R)]
+
+UP, LA, LB, PE, PL, GL, SB = 0, 8, 48, 88, 136, 168, 170
+(P_R, P_PAR, P_R1, P_RH, P_RQ, P_T1, P_T2, P_W, P_D, P_IP, P_A, P_B, P_MA, P_MB, P_OE, P_OL, P_HE, P_HL, P_S0, P_S1,
+ P_X, P_X2, P_R16, P_OL0, P_P2) = range(25)
+NA, RG, BQ, S0, S1, EE, EL, SL0, SL1, FG = 1, "vava", "vava", "aa", "aa", "aava", "vava", "av", "av", "avav"
+
+
+def rank_program(g, core, T, topo):
+    rank = T.rank_of(core)
+    if rank is None:
+        return
+    N = len(T.cores)
+    Q = {"v": g.vector, "a": g.scalar, "p": g.tensor, "g": g, "s": g.sync}
+    SEM = {"v": "nv", "a": "na", "p": "np_", "g": "ng"}
+    count = {k: 0 for k in SEM}
+    known = {k: {} for k in Q}
+    hist = {}
+    total = {}
+
+    def v(name, c0, c1, st=1, p0=0, p1=128):
+        return (name if name in SCRATCH else "b_" + name, c0, c1, st, p0, p1)
+
+    def ap(w):
+        return T[w[0]][w[4]:w[5], w[1]:w[2]:w[3]] if w[3] != 1 else T[w[0]][w[4]:w[5], w[1]:w[2]]
+
+    def foot(w):
+        cols = 0
+        for c in range(w[1], w[2], w[3]):
+            cols |= 1 << c
+        banks = 0
+        if w[0] in ("pa", "pb"):
+            for k in range(w[1] // 512, (w[2] - 1) // 512 + 1):
+                banks |= 1 << k
+        return cols, ((1 << w[5]) - 1) ^ ((1 << w[4]) - 1), banks
+
+    def wait(q, sem, n, more=None):
+        if known[q].get(sem, 0) < n:
+            Q[q].wait_ge(T.sem[sem], n)
+            known[q][sem] = n
+        for s2, n2 in (more or {}).items():
+            if known[q].get(s2, 0) < n2:
+                known[q][s2] = n2
+
+    def op(q, fn, reads, writes, dma=None, after=(), chain=False):
+        need = {}
+        acc = [(w, False) for w in reads] + [(w, True) for w in writes]
+        feet = [(w[0], wr) + foot(w) for w, wr in acc]
+        for name, wr, cols, parts, banks in feet:
+            for q2, sem, n, wr2, cols2, parts2, banks2, kn in hist.get(name, ()):
+                hit = (wr or wr2) and (cols & cols2) and (parts & parts2)
+                if q2 != q and (banks & banks2):
+                    hit = True
+                if chain and q2 == q and banks2:
+                    hit = False
+                if hit and need.get(sem, (0, None))[0] < n:
+                    need[sem] = (n, kn)
+        for sem, n in after:
+            wait(q, sem, n)
+        todo = sorted(need.items(), key=lambda e: -len(e[1][1]))
+        for sem, (n, kn) in todo:
+            wait(q, sem, n, kn)
+        ins = fn()
+        if dma == "remote":
+            return
+        if dma:
+            ins.then_inc(T.sem[dma], 16)
+            sem, n = dma, 16
+        else:
+            count[q] += 1
+            sem, n = SEM[q], count[q]
+            ins.then_inc(T.sem[sem], 1)
+        total[sem] = n
+        kn = dict(known[q])
+        for name, wr, cols, parts, banks in feet:
+            hist.setdefault(name, []).append((q if not dma else dma, sem, n, wr, cols, parts, banks, kn))
+
+    def sc(x):
+        return ap(x) if isinstance(x, tuple) else x
+
+    def tl(*xs):
+        return [x for x in xs if isinstance(x, tuple)]
+
+    def src(w, off):
+        return ap(w) if off is None else ap(w).indirect(ap(off))
+
+    def copy(q, out, in_, off=None, after=()):
+        if q == "v":
+            op(q, lambda: g.vector.tensor_copy(ap(out), src(in_, off)), tl(in_, off), [out], after=after)
+        else:
+            op(q, lambda: g.scalar.activation(ap(out), src(in_, off), ACT.Copy), tl(in_, off), [out], after=after)
+
+    def scatter(win, off, in_):
+        op("v", lambda: g.vector.tensor_copy(ap(win).indirect(ap(off)), ap(in_)), [in_, off], [win])
+
+    def ts(out, in_, s1, op0, s2=None, op1=None, off=None):
+        if op1 is None:
+            op("v", lambda: g.vector.tensor_scalar(ap(out), src(in_, off), sc(s1), None, op0), tl(in_, off, s1), [out])
+        else:
+            op("v", lambda: g.vector.tensor_scalar(ap(out), src(in_, off), sc(s1), sc(s2), op0, op1),
+               tl(in_, off, s1, s2), [out])
+
+    def tt(out, a, b, o, off=None):
+        op("v", lambda: g.vector.tensor_tensor(ap(out), src(a, off), ap(b), o), tl(a, b, off), [out])
+
+    def act(out, in_, f, bias=0.0, scale=1.0, acc=None, off=None):
+        if acc is None:
+            op("a", lambda: g.scalar.activation(ap(out), src(in_, off), f, bias=sc(bias), scale=sc(scale)),
+               tl(in_, bias, scale, off), [out])
+        else:
+            op("a", lambda: g.scalar.activation(ap(out), ap(in_), f, accum_out=ap(acc)), [in_], [out, acc])
+
+    def fill(w, c):
+        op("v", lambda: g.vector.memset(ap(w), c), [], [w])
+
+    def turn(out, in_):
+        op("v", lambda: g.vector.transpose(ap(out), ap(in_)), [in_], [out])
+
+    def iota(out, pat, base=0, cm=0):
+        if SCRATCH[out[0]][2] == I32:
+            op("g", lambda: g.iota(ap(out), pat, base, cm), [], [out])
+        else:
+            op("g", lambda: g.iota(ap(out), pat, base, cm, allow_small_or_imprecise_dtypes=True), [], [out])
+
+    def quant(name, c0, tile, t0, n):
+        o, s, i = v("q" + name, c0, c0 + n), v("s" + name, c0, c0 + n), v(tile, t0, t0 + 4 * n)
+        op("v", lambda: g.vector.quantize_mx(ap(o), ap(s), ap(i)), [i], [o, s])
+
+    def mm(ps, bank, a, a0, b, b0, n, start=True, stop=True, after=()):
+        o = v(ps, 512 * bank, 512 * bank + n)
+        w = [v("q" + a, a0, a0 + 128), v("s" + a, a0, a0 + 128), v("q" + b, b0, b0 + n), v("s" + b, b0, b0 + n)]
+        op("p", lambda: g.tensor.matmul_mx(ap(o), ap(w[0]), ap(w[1]), ap(w[2]), ap(w[3]), start, stop), w, [o],
+           after=after, chain=not start)
+
+    def pick(dst, d0, n, win, w0, w1, off):
+        o, i = v("q" + dst, d0, d0 + n), v("q" + win, w0, w1)
+        op("v", lambda: g.vector.tensor_copy(ap(o).bitcast(dt.uint32), ap(i).bitcast(dt.uint32).indirect(ap(off))),
+           [i, off], [o])
+        copy("a", v("s" + dst, d0, d0 + n), v("s" + win, w0, w1), off)
+
+    def dma(q, sem, out, in_, reads, writes, after=()):
+        op(q, lambda: Q[q].dma_start(out, in_), reads, writes, dma=sem, after=after)
+
+    sent = [0]
+
+    def peer(t, sign):
+        return T.cores[(rank + sign * (1 + t)) % N]
+
+    def send(t, out, in_, sem):
+        dst = peer(t, 1)
+        rid, pid = topo.addr(dst)[:2]
+        a, b = ap(out), ap(in_)
+        if SCRATCH[out[0]][2] == QX:
+            a, b = a.bitcast(dt.uint8), b.bitcast(dt.uint8)
+        op("g", lambda: g.remote_dma(a, b, T.sem[sem], T.sem["sent"], pid, rid, topo.mask(core, dst)), [in_], [],
+           dma="remote")
+        sent[0] += len(topo.engines(core, dst))
+
+    def send_codes(t, name, n, at):
+        send(t, v("qg%d" % t, at, at + n), v("q" + name, 0, n), "ag%d" % t)
+        send(t, v("sg%d" % t, at, at + n), v("s" + name, 0, n), "ag%d" % t)
+
+    def lands(t, calls):
+        return calls * len(topo.engines(peer(t, -1), core))
+
+    def pc(k, p0=0, p1=128):
+        return v("pc", k, k + 1, 1, p0, p1)
+
+    def lu(a, n):
+        return v("lu", a, a + n)
+
+    ID = ACT.Identity
+
+    def ranks(k, mid=None):
+        turn(v("xtt", 0, 160), v("row", 16, 176))
+        turn(v("xtt", 160, 352), v("row", 0, 192))
+        copy("v", v("col", 0, 16), v("xtt", 0, 352), lu(GL, 1))
+        if NA:
+            act(v("ncol", 0, 16), v("xtt", 0, 352), ACT.Copy, 0.0, -1.0, off=lu(GL, 1))
+        for c in range(NA):
+            act(v("cm", 176 * c + 16, 160 * c + 160), v("row", 32 + 16 * c, 176), ACT.Sign, v("ncol", c, c + 1))
+        for c in range(10):
+            ts(v("cm", 160 * c, 176 * c + 16), v("row", 16, 32 + 16 * c), v("col", c, c + 1), ALU.is_ge)
+            if NA <= c < 9:
+                ts(v("cm", 176 * c + 16, 160 * c + 160), v("row", 32 + 16 * c, 176), v("col", c, c + 1), ALU.is_gt)
+            act(v("cm", 160 * c, 160 * c + 160), v("cm", 160 * c, 160 * c + 160), ACT.Relu, acc=v("acc", c, c + 1))
+        tt(v("db", 0, C), v("xtt", 0, 352), v("row", 16, 176), ALU.is_equal, off=lu(SB, 10))
+        op("v", lambda: g.vector.tensor_tensor_scan(ap(v("dc", 0, C)), ap(v("db", 0, C)), ap(v("rst", 0, C)), 0.0,
+                                                    ALU.add, ALU.mult),
+           [v("rst", 0, C), v("db", 0, C)], [v("dc", 0, C)])
+        if mid:
+            mid()
+        rk = v("rk%d" % (k % 2), 0, 10)
+        tt(rk, v("acc", 0, 10), v("dc", 15, C, 16), ALU.subtract)
+        ts(v("ru", 0, 10), rk, -1.0, ALU.add)
+
+    def invert(k):
+        scatter(v("inv", 16, 176), v("ru", 0, 10), v("ir" if k < 2 else "val%d" % (k % 2), 0, C))
+        n = C if k == 0 else KEEP
+        turn(v("tt", 0, n), v("inv", 16, 16 + n))
+        turn(v("tt", 160, 192 + n), v("inv", 0, 32 + n))
+        copy("v", v("ls%d" % k, 0, 16), v("tt", 0, 352), lu(GL, 1))
+        if k > 0:
+            send(k - 1, v("ll%d" % (k - 1), 0, 4), v("ls%d" % k, 0, 4), "al%d" % (k - 1))
+
+    def keep_rank(k):
+        ts(v("rs", 0, 10), v("rk%d" % (k % 2), 0, 10), 2.0, ALU.mult, pc(P_P2), ALU.add)
+
+    def keep_val(k):
+        if 0 < k < R:
+            copy("a", v("val%d" % ((k + 1) % 2), 0, C), v("ir", 0, C), v("ru", 0, 10))
+
+    def regather(out, win, step, width, n, lst, qs):
+        for t in range(4):
+            copy(qs[t], v(out, t, 4 * n, 4), v(win, step * t, step * t + width), v(lst, 0, n // 16))
+
+    def flat(at, n):
+        for b in range(4):
+            copy("a", v("sp", PL_W * b + at, PL_W * b + at + n), v("si", 4 * at + b, 4 * (at + n), 4))
+
+    def unpack(name, n, after=()):
+        for b in range(4):
+            mm("pa", b, "e", 128 * b, name, 0, n, after=after)
+
+    def evac(out, at, n, planar, qs):
+        for b in range(4):
+            o = v(out, C * b, C * b + n) if planar else v(out, 4 * at + b, 4 * (at + n), 4)
+            copy(qs[b], o, v("pa", 512 * b, 512 * b + n))
+
+    def theirs(t):
+        unpack("g%d" % t, C, after=[("ag%d" % t, lands(t, 2 if t == 0 else 4))])
+        evac("gp", 0, C, True, "aaaa")
+
+    def ab_early():
+        copy("a", v("abe", 384, 768), v("si", 0, 384), lu(LB, 24))
+        quant("ab", 192, "si", 0, 128)
+        copy("v", v("abe", 0, 384), v("si", 0, 384), lu(LA, 24))
+        quant("ab", 0, "abe", 0, 192)
+
+    def ab_late():
+        copy("v", v("abl", 0, 256), v("si", 0, 640), lu(LA + 24, 16))
+        copy("a", v("abl", 256, 512), v("si", 0, 640), lu(LB + 24, 16))
+        quant("ab", 320, "abl", 0, 128)
+
+    def trial(late, h):
+        n, name, ps = (128, "yl", "pa") if late else (192, "ye", "pb")
+        if late:
+            pick(name, 2 * n * h, 2 * n, "ab", 192, 448, lu(PL + 16 * h, 16))
+        else:
+            pick(name, 2 * n * h, 2 * n, "ab", 0, 320, lu(PE + 24 * h, 24))
+        for k in (2 * h, 2 * h + 1):
+            mm(ps, k, "up", 0, name, n * k, n)
+
+    def scores(late, h, qs):
+        n, at, ps = (128, 192, "pa") if late else (192, 0, "pb")
+        for k in (2 * h, 2 * h + 1):
+            copy(qs[k % 2], v("xs", at, at + n, 1, 32 * k, 32 * k + 32), v(ps, 512 * k, 512 * k + n, 1, 32 * k, 32 * k + 32))
+
+    def to_row():
+        copy("v", v("row", 16, 112), v("xs", 0, 320), v("rs", 0, 6))
+        copy("a", v("row", 112, 176), v("xs", 0, 320), v("rs", 6, 10))
+
+    def take(t):
+        for b in range(4):
+            copy(BQ[b], v("bt", b, 256, 4), v("gp", C * b, C * b + C), v("ll%d" % t, 0, 4),
+                 after=[("al%d" % t, lands(t, 1))])
+        quant("b", 64, "bt", 0, 128)
+        for b in range(4):
+            mm("pa", b, "w", 128 * b, "b", 64, 128, True, False)
+            mm("pa", b, "e", 128 * b, "b", 0, 128, False, True)
+
+    def layer(last):
+        for b in range(4):
+            act(v("rl", 64 * b, 64 * b + 64), v("pa", 512 * b, 512 * b + 64), ACT.Relu, 0.0, 0.03125)
+            tt(v("sp", PL_W * b + C, PL_W * (b + 1)) if last else v("kl", b, 256, 4),
+               v("rl", 64 * b, 64 * b + 64), v("pa", 512 * b + 64, 512 * b + 128), ALU.add)
+
+    dma("a", "du", ap(v("ut", 0, 512)), T.u[:], [], [v("ut", 0, 512)])
+    dma("s", "dx", ap(v("xt", 0, 640)), T.x[:], [], [v("xt", 0, 640)])
+    iota(v("pi", 0, 1), [[0, 1]], 0, 1)
+    iota(v("up", 0, 8), [[16, 8]])
+    iota(v("c40", 0, 40), [[1, 40]])
+    iota(v("lt", PE, PE + 48), [[0, 4], [4, 12]])
+    iota(v("lt", PL, PL + 32), [[0, 4], [4, 8]])
+    fill(v("ones", 0, 516), 1.0)
+    p_ = v("pi", 0, 1)
+    AND, SHR = ALU.bitwise_and, ALU.logical_shift_right
+    ts(v("pi", 1, 2), p_, 15, AND)
+    ts(v("pi", 2, 3), p_, 4, SHR, 1, AND)
+    ts(v("pi", 3, 4), p_, 1, AND)
+    ts(v("pi", 4, 5), p_, 15, AND, 1, SHR)
+    ts(v("pi", 5, 6), p_, 15, AND, 2, SHR)
+    ts(v("pi", 6, 7), p_, 8, AND, 1, SHR)
+    ts(v("pi", 7, 8), p_, 3, AND)
+    copy("v", lu(UP, 8), v("up", 0, 8))
+    copy("v", v("pc", 0, 7), v("pi", 1, 8))
+    op("g", lambda: g.affine_select(ap(v("et", 0, 516)), ap(v("ones", 0, 516)), [[-1, 516]], ALU.is_equal, 0.0, 3, 4),
+       [v("ones", 0, 516)], [v("et", 0, 516)])
+    iota(v("q16", 0, C), [[0, 10], [1, 16]])
+    iota(v("ir", 0, C), [[1, C]])
+    fill(v("kl", 0, 512), 0.0)
+    fill(v("ke", 384, 512), 0.0)
+    fill(v("bt", 256, 512), 0.0)
+    quant("b", 0, "kl", 0, 128)
+    act(pc(P_X), pc(P_PAR), ID, pc(P_R1), -1.0)
+    act(pc(P_R16), pc(P_R), ID, 0.0, 16.0)
+    act(pc(P_S0), pc(P_PAR), ID, 0.0, 176.0)
+    act(pc(P_S1), pc(P_PAR), ID, 192.0, -176.0)
+    act(pc(P_X2), pc(P_X), ACT.Square)
+    act(v("lt", SB, SB + 10, 2), v("c40", 0, 5), ID, pc(P_S0), 32.0)
+    act(v("lt", SB + 1, SB + 10, 2), v("c40", 0, 5), ID, pc(P_S1), 32.0)
+    act(v("lt", GL, GL + 1), pc(P_X2), ID, pc(P_R16), 176.0)
+    act(pc(P_W), pc(P_T1), ID, pc(P_T2))
+    act(pc(P_IP), pc(P_PAR), ID, 1.0, -1.0)
+    act(pc(P_MA), pc(P_PAR), ID, 16.0, -8.0)
+    act(pc(P_MB), pc(P_PAR), ID, 8.0, 8.0)
+    act(pc(P_D), pc(P_R), ID, pc(P_W), -1.0)
+    act(pc(P_OE), pc(P_R1), ID, pc(P_RH), 96.0)
+    act(pc(P_OL0), pc(P_R1), ID, pc(P_RH), 64.0)
+    act(pc(P_HE), pc(P_RQ), ID, 192.0)
+    act(pc(P_HL), pc(P_RQ), ID, 48.0)
+    act(pc(P_A), pc(P_PAR), ID, pc(P_R), pc(P_D))
+    act(pc(P_B), pc(P_IP), ID, pc(P_R), pc(P_D))
+    act(pc(P_OL), pc(P_OL0), ID, 128.0)
+    act(pc(P_P2), pc(P_PAR), ID, -2.0)
+    fill(v("row", 0, 16), 0.0)
+    fill(v("row", 176, 192), 0.0)
+    fill(v("inv", 0, 192), 0.0)
+    ts(lu(GL, 1), v("lt", GL, GL + 1), 351.0, ALU.min)
+    copy("v", lu(SB, 10), v("lt", SB, SB + 10))
+    act(v("lt", PE, PE + 48), v("lt", PE, PE + 48), ID, pc(P_HE))
+    act(v("lt", PL, PL + 32), v("lt", PL, PL + 32), ID, pc(P_HL))
+    act(v("lt", LA, LA + 40), v("c40", 0, 40), ID, pc(P_A), pc(P_MA))
+    act(v("lt", LB, LB + 40), v("c40", 0, 40), ID, pc(P_B), pc(P_MB))
+
+    def own_lists(k):
+        a, z = 32 * k, 32 * k + 32
+        act(v("lt", PE + 12 * k, PE + 12 * k + 12, 1, a, z), v("c40", 0, 12, 1, a, z), ID, pc(P_OE, a, z), 8.0)
+        act(v("lt", PL + 8 * k, PL + 8 * k + 8, 1, a, z), v("c40", 0, 8, 1, a, z), ID, pc(P_OL, a, z), 8.0)
+    own_lists(0)
+    own_lists(1)
+    quant("e", 0, "et", 3, 128)
+    quant("e", 128, "et", 2, 128)
+    quant("u", 0, "ut", 0, 128)
+    pick("up", 0, 128, "u", 0, 128, lu(UP, 8))
+    quant("x", 0, "xt", 0, C)
+    mm("pb", 0, "up", 0, "x", 0, C)
+    send_codes(0, "x", C, 0)
+    dma("s", "dwc", ap(v("qw", 0, 512)).bitcast(dt.uint8), T.wc[:], [], [v("qw", 0, 512)], after=[("dx", 16), ("du", 16)])
+    dma("s", "dws", ap(v("sw", 0, 512)), T.ws[:], [], [v("sw", 0, 512)])
+    dma("s", "dv", ap(v("vt", 0, 512)), T.v[:], [], [v("vt", 0, 512)])
+    own_lists(2)
+    own_lists(3)
+    quant("e", 256, "et", 1, 128)
+    quant("e", 384, "et", 0, 128)
+    copy("a", v("row", 16, 176), v("pb", 0, C))
+    ts(v("rst", 0, C), v("q16", 0, C), pc(P_R), ALU.is_gt)
+    unpack("x", C)
+
+    def first_mid():
+        evac("t0", 0, C, True, "aaaa")
+        copy("v", lu(LA, PL + 32 - LA), v("lt", LA, PL + 32))
+    ranks(0, first_mid)
+    invert(0)
+    regather("si", "t0", C, C, C, "ls0", "vava")
+    ab_early()
+    keep_rank(0)
+    trial(False, 0)
+    ab_late()
+    trial(False, 1)
+    scores(False, 0, "av")
+    trial(True, 0)
+    scores(False, 1, "av")
+    trial(True, 1)
+    scores(True, 0, "av")
+    scores(True, 1, "av")
+    to_row()
+
+    for t in range(R):
+        k = t + 1
+        ranks(k, lambda: theirs(t))
+        keep_val(k)
+        invert(k)
+        if k == R:
+            break
+        regather("ke", "sp" if t else "t0", PL_W if t else C, C, KEEP, "ls%d" % k, RG)
+        quant("se%d" % k, 0, "ke", 0, 128)
+        unpack("se%d" % k, 128)
+        send_codes(k, "se%d" % k, KEEP, 0)
+        keep_rank(k)
+        evac("si", 0, KEEP, False, EE)
+        ab_early()
+        flat(0, KEEP)
+        trial(False, 0)
+        take(t)
+        trial(False, 1)
+        layer(False)
+        quant("sl%d" % k, 0, "kl", 0, 128)
+        unpack("sl%d" % k, 128)
+        send_codes(k, "sl%d" % k, M, KEEP)
+        scores(False, 0, S0)
+        evac("si", KEEP, M, False, EL)
+        ab_late()
+        scores(False, 1, S1)
+        trial(True, 0)
+        trial(True, 1)
+        scores(True, 0, SL0)
+        scores(True, 1, SL1)
+        to_row()
+        flat(KEEP, M)
+
+    new, old = v("rk%d" % (R % 2), 0, 10), v("rk%d" % ((R - 1) % 2), 0, 10)
+    f1, f2, f3, f4 = (v("f%d" % i, 0, 10) for i in (1, 2, 3, 4))
+    tt(f1, new, old, ALU.subtract)
+    ts(f2, new, float(KEEP), ALU.is_gt)
+    scatter(v("olr", 0, C), v("ru", 0, 10), v("ir", 0, C))
+    ts(f3, f1, float(C - KEEP), ALU.add)
+    quant("v", 0, "vt", 0, 128)
+    tt(f1, f3, f2, ALU.mult)
+    dma("s", "dol", T.ol[:], T["b_olr"][0:128:16, 0:C], [v("olr", 0, C)], [])
+    tt(f4, f1, old, ALU.add)
+    ts(v("fl", 0, 10), f4, -1.0, ALU.add)
+    take(R - 1)
+    layer(True)
+    regather("tf", "sp", PL_W, PL_W, C, "fl", FG)
+    quant("f", 0, "tf", 0, C)
+    mm("pb", 0, "v", 0, "f", 0, C)
+    dma("s", "doc", T.oc[:], ap(v("qf", 0, C)).bitcast(dt.uint8), [v("qf", 0, C)], [])
+    for k in range(4):
+        w = v("sf", 0, C, 1, 32 * k, 32 * k + 4)
+        dma("sa"[k % 2], "ds%d" % k, T.osc[4 * k:4 * k + 4, 0:C], ap(w), [w], [])
+    copy("v", v("yo", 0, C), v("pb", 0, C))
+    dma("a", "dy", T.y[:], ap(v("yo", 0, C)), [v("yo", 0, C)], [])
+
+    wait("g", "sent", sent[0])
+    for sem, n in total.items():
+        if max(known[q].get(sem, 0) for q in Q) < n or sem in SEM.values():
+            wait("s", sem, n)

@@ -1,4 +1,4 @@
-from concourse.mybir import dt, AluOpType, ActivationFunctionType
+from concourse.mybir import dt, AluOpType, ActivationFunctionType, AxisListType
 
 ALU = AluOpType
 ACT = ActivationFunctionType
@@ -51,7 +51,8 @@ SEMAPHORES = ["nv", "na", "np_", "ng", "sent"] + DMAS + ["ag%d" % t for t in ran
 UP, LA, LB, PE, PL, GL, SB = 0, 8, 48, 88, 136, 168, 170
 (P_R, P_PAR, P_R1, P_RH, P_RQ, P_T1, P_T2, P_W, P_D, P_IP, P_A, P_B, P_MA, P_MB, P_OE, P_OL, P_HE, P_HL, P_S0, P_S1,
  P_X, P_X2, P_R16, P_OL0, P_P2) = range(25)
-NA, RG, BQ, S0, S1, EE, EL, SL0, SL1, FG = 1, "vava", "vava", "aa", "aa", "aava", "vava", "av", "av", "avav"
+NA, RG, BQ, S0, S1, EE, EL, SL0, SL1, FG = 2, "vava", "vava", "av", "av", "vava", "vava", "av", "av", "avav"
+FE, FL = "aaaa", "vava"
 
 
 def rank_program(g, core, T, topo):
@@ -222,20 +223,25 @@ def rank_program(g, core, T, topo):
     def ranks(k, mid=None):
         turn(v("xtt", 0, 160), v("row", 16, 176))
         turn(v("xtt", 160, 352), v("row", 0, 192))
+        if k == 0:
+            quant("e", 384, "et", 0, 128)
+            unpack("x", C)
         copy("v", v("col", 0, 16), v("xtt", 0, 352), lu(GL, 1))
-        if NA:
-            act(v("ncol", 0, 16), v("xtt", 0, 352), ACT.Copy, 0.0, -1.0, off=lu(GL, 1))
+        tt(v("db", 0, C), v("xtt", 0, 352), v("row", 16, 176), ALU.is_equal, off=lu(SB, 10))
+        act(v("ncol", 0, 16), v("xtt", 0, 352), ACT.Copy, 0.0, -1.0, off=lu(GL, 1))
         for c in range(NA):
             act(v("cm", 176 * c + 16, 160 * c + 160), v("row", 32 + 16 * c, 176), ACT.Sign, v("ncol", c, c + 1))
-        for c in range(10):
+        for c in range(9):
             ts(v("cm", 160 * c, 176 * c + 16), v("row", 16, 32 + 16 * c), v("col", c, c + 1), ALU.is_ge)
-            if NA <= c < 9:
+            if NA <= c:
                 ts(v("cm", 176 * c + 16, 160 * c + 160), v("row", 32 + 16 * c, 176), v("col", c, c + 1), ALU.is_gt)
             act(v("cm", 160 * c, 160 * c + 160), v("cm", 160 * c, 160 * c + 160), ACT.Relu, acc=v("acc", c, c + 1))
-        tt(v("db", 0, C), v("xtt", 0, 352), v("row", 16, 176), ALU.is_equal, off=lu(SB, 10))
+        ts(v("cm", 1440, 1600), v("row", 16, 176), v("col", 9, 10), ALU.is_ge)
         op("v", lambda: g.vector.tensor_tensor_scan(ap(v("dc", 0, C)), ap(v("db", 0, C)), ap(v("rst", 0, C)), 0.0,
                                                     ALU.add, ALU.mult),
            [v("rst", 0, C), v("db", 0, C)], [v("dc", 0, C)])
+        op("v", lambda: g.vector.tensor_reduce(ap(v("acc", 9, 10)), ap(v("cm", 1440, 1600)), AxisListType.X, ALU.add),
+           [v("cm", 1440, 1600)], [v("acc", 9, 10)])
         if mid:
             mid()
         rk = v("rk%d" % (k % 2), 0, 10)
@@ -244,6 +250,10 @@ def rank_program(g, core, T, topo):
 
     def invert(k):
         scatter(v("inv", 16, 176), v("ru", 0, 10), v("ir" if k < 2 else "val%d" % (k % 2), 0, C))
+        if k == 0:
+            copy("v", lu(LA, PL + 32 - LA), v("lt", LA, PL + 32))
+        if k == 1:
+            quant("b", 0, "kl", 0, 128)
         n = C if k == 0 else KEEP
         turn(v("tt", 0, n), v("inv", 16, 16 + n))
         turn(v("tt", 160, 192 + n), v("inv", 0, 32 + n))
@@ -262,9 +272,9 @@ def rank_program(g, core, T, topo):
         for t in range(4):
             copy(qs[t], v(out, t, 4 * n, 4), v(win, step * t, step * t + width), v(lst, 0, n // 16))
 
-    def flat(at, n):
+    def flat(at, n, qs):
         for b in range(4):
-            copy("a", v("sp", PL_W * b + at, PL_W * b + at + n), v("si", 4 * at + b, 4 * (at + n), 4))
+            copy(qs[b], v("sp", PL_W * b + at, PL_W * b + at + n), v("si", 4 * at + b, 4 * (at + n), 4))
 
     def unpack(name, n, after=()):
         for b in range(4):
@@ -346,10 +356,6 @@ def rank_program(g, core, T, topo):
        [v("ones", 0, 516)], [v("et", 0, 516)])
     iota(v("q16", 0, C), [[0, 10], [1, 16]])
     iota(v("ir", 0, C), [[1, C]])
-    fill(v("kl", 0, 512), 0.0)
-    fill(v("ke", 384, 512), 0.0)
-    fill(v("bt", 256, 512), 0.0)
-    quant("b", 0, "kl", 0, 128)
     act(pc(P_X), pc(P_PAR), ID, pc(P_R1), -1.0)
     act(pc(P_R16), pc(P_R), ID, 0.0, 16.0)
     act(pc(P_S0), pc(P_PAR), ID, 0.0, 176.0)
@@ -358,19 +364,12 @@ def rank_program(g, core, T, topo):
     act(v("lt", SB, SB + 10, 2), v("c40", 0, 5), ID, pc(P_S0), 32.0)
     act(v("lt", SB + 1, SB + 10, 2), v("c40", 0, 5), ID, pc(P_S1), 32.0)
     act(v("lt", GL, GL + 1), pc(P_X2), ID, pc(P_R16), 176.0)
-    act(pc(P_W), pc(P_T1), ID, pc(P_T2))
-    act(pc(P_IP), pc(P_PAR), ID, 1.0, -1.0)
-    act(pc(P_MA), pc(P_PAR), ID, 16.0, -8.0)
-    act(pc(P_MB), pc(P_PAR), ID, 8.0, 8.0)
-    act(pc(P_D), pc(P_R), ID, pc(P_W), -1.0)
-    act(pc(P_OE), pc(P_R1), ID, pc(P_RH), 96.0)
-    act(pc(P_OL0), pc(P_R1), ID, pc(P_RH), 64.0)
-    act(pc(P_HE), pc(P_RQ), ID, 192.0)
-    act(pc(P_HL), pc(P_RQ), ID, 48.0)
-    act(pc(P_A), pc(P_PAR), ID, pc(P_R), pc(P_D))
-    act(pc(P_B), pc(P_IP), ID, pc(P_R), pc(P_D))
-    act(pc(P_OL), pc(P_OL0), ID, 128.0)
-    act(pc(P_P2), pc(P_PAR), ID, -2.0)
+    for o, i, scale, bias in (
+            (P_W, P_T1, 1.0, pc(P_T2)), (P_IP, P_PAR, -1.0, 1.0), (P_MA, P_PAR, -8.0, 16.0), (P_MB, P_PAR, 8.0, 8.0),
+            (P_D, P_R, -1.0, pc(P_W)), (P_OE, P_R1, 96.0, pc(P_RH)), (P_OL0, P_R1, 64.0, pc(P_RH)),
+            (P_HE, P_RQ, 1.0, 192.0), (P_HL, P_RQ, 1.0, 48.0), (P_A, P_PAR, pc(P_D), pc(P_R)),
+            (P_B, P_IP, pc(P_D), pc(P_R)), (P_OL, P_OL0, 1.0, 128.0), (P_P2, P_PAR, 1.0, -2.0)):
+        ts(pc(o), pc(i), scale, ALU.mult, bias, ALU.add)
     fill(v("row", 0, 16), 0.0)
     fill(v("row", 176, 192), 0.0)
     fill(v("inv", 0, 192), 0.0)
@@ -387,28 +386,26 @@ def rank_program(g, core, T, topo):
         act(v("lt", PL + 8 * k, PL + 8 * k + 8, 1, a, z), v("c40", 0, 8, 1, a, z), ID, pc(P_OL, a, z), 8.0)
     own_lists(0)
     own_lists(1)
-    quant("e", 0, "et", 3, 128)
-    quant("e", 128, "et", 2, 128)
     quant("u", 0, "ut", 0, 128)
     pick("up", 0, 128, "u", 0, 128, lu(UP, 8))
     quant("x", 0, "xt", 0, C)
     mm("pb", 0, "up", 0, "x", 0, C)
     send_codes(0, "x", C, 0)
+    iota(v("kl", 0, 512), [[0, 512]])
+    iota(v("ke", 384, 512), [[0, 128]])
+    iota(v("bt", 256, 512), [[0, 256]])
     dma("s", "dwc", ap(v("qw", 0, 512)).bitcast(dt.uint8), T.wc[:], [], [v("qw", 0, 512)], after=[("dx", 16), ("du", 16)])
     dma("s", "dws", ap(v("sw", 0, 512)), T.ws[:], [], [v("sw", 0, 512)])
     dma("s", "dv", ap(v("vt", 0, 512)), T.v[:], [], [v("vt", 0, 512)])
     own_lists(2)
     own_lists(3)
+    quant("e", 0, "et", 3, 128)
+    quant("e", 128, "et", 2, 128)
     quant("e", 256, "et", 1, 128)
-    quant("e", 384, "et", 0, 128)
     copy("a", v("row", 16, 176), v("pb", 0, C))
     ts(v("rst", 0, C), v("q16", 0, C), pc(P_R), ALU.is_gt)
-    unpack("x", C)
 
-    def first_mid():
-        evac("t0", 0, C, True, "aaaa")
-        copy("v", lu(LA, PL + 32 - LA), v("lt", LA, PL + 32))
-    ranks(0, first_mid)
+    ranks(0, lambda: evac("t0", 0, C, True, "aaaa"))
     invert(0)
     regather("si", "t0", C, C, C, "ls0", "vava")
     ab_early()
@@ -438,16 +435,16 @@ def rank_program(g, core, T, topo):
         keep_rank(k)
         evac("si", 0, KEEP, False, EE)
         ab_early()
-        flat(0, KEEP)
-        trial(False, 0)
+        flat(0, KEEP, FE)
         take(t)
-        trial(False, 1)
+        trial(False, 0)
         layer(False)
         quant("sl%d" % k, 0, "kl", 0, 128)
         unpack("sl%d" % k, 128)
         send_codes(k, "sl%d" % k, M, KEEP)
-        scores(False, 0, S0)
+        trial(False, 1)
         evac("si", KEEP, M, False, EL)
+        scores(False, 0, S0)
         ab_late()
         scores(False, 1, S1)
         trial(True, 0)
@@ -455,7 +452,7 @@ def rank_program(g, core, T, topo):
         scores(True, 0, SL0)
         scores(True, 1, SL1)
         to_row()
-        flat(KEEP, M)
+        flat(KEEP, M, FL)
 
     new, old = v("rk%d" % (R % 2), 0, 10), v("rk%d" % ((R - 1) % 2), 0, 10)
     f1, f2, f3, f4 = (v("f%d" % i, 0, 10) for i in (1, 2, 3, 4))

from concourse.mybir import dt, AluOpType, ActivationFunctionType, AxisListType

ALU = AluOpType
ACT = ActivationFunctionType
C, M, R, KEEP = 160, 64, 3, 96
PL_W = C + M
BF, F32, I32, U16, QX, U8 = "bfloat16", "float32", "int32", "uint16", "float8_e4m3fn_x4", "uint8"


def _scratch():
    s = {}

    def b(name, n, d, where="sbuf"):
        s[name] = (where, [128, n], d)

    def q(name, n):
        b("q" + name, n, QX)
        b("s" + name, n, U8)
    for name, n in (("xt", 640), ("ut", 512), ("vt", 512), ("et", 516), ("ones", 516), ("t0", 640), ("si", 640),
                    ("sp", 4 * PL_W), ("ke", 512), ("kl", 512), ("abe", 768), ("abl", 512), ("gp", 640), ("bt", 512),
                    ("tf", 640), ("cm", 1600), ("db", 160), ("dc", 160), ("rst", 160),
                    ("ir", 160), ("val0", 160), ("val1", 160), ("inv", 192), ("tt", 352)):
        b("b_" + name, n, BF)
    for name, n in (("pc", 32), ("c40", 40), ("q16", 160), ("lt", 180), ("xs", 320), ("row", 192), ("xtt", 352),
                    ("col", 16), ("ncol", 16), ("acc", 10), ("rk0", 10), ("rk1", 10), ("rl", 256), ("olr", 160),
                    ("yo", 160), ("f1", 10), ("f2", 10), ("f3", 10), ("f4", 10)):
        b("b_" + name, n, F32)
    b("b_pi", 8, I32)
    b("b_up", 8, I32)
    for name, n in (("lu", 180), ("ru", 10), ("rs", 10), ("fl", 10), ("ls3", 16)):
        b("b_" + name, n, U16)
    for t in range(R):
        b("b_ls%d" % t, 16, U16)
        b("b_ll%d" % t, 4, U16)
        q("g%d" % t, C)
    for t in (1, 2):
        q("se%d" % t, 128)
        q("sl%d" % t, 128)
    for name, n in (("x", C), ("u", 128), ("up", 128), ("v", 128), ("w", 512), ("e", 512), ("ab", 448), ("ye", 768),
                    ("yl", 512), ("b", 192), ("f", C)):
        q(name, n)
    b("pa", 2048, F32, "psum")
    b("pb", 2048, F32, "psum")
    return s


SCRATCH = _scratch()
DMAS = ["dx", "du", "dv", "dwc", "dws", "dol", "doc", "ds0", "ds1", "ds2", "ds3", "dy"]
SEMAPHORES = ["nv", "na", "np_", "ng", "sent"] + DMAS + ["ag%d" % t for t in range(R)] + ["al%d" % t for t in range(R)]

UP, LA, LB, PE, PL, GL, SB = 0, 8, 48, 88, 136, 168, 170
(P_R, P_PAR, P_R1, P_RH, P_RQ, P_T1, P_T2, P_W, P_D, P_IP, P_A, P_B, P_MA, P_MB, P_OE, P_OL, P_HE, P_HL, P_S0, P_S1,
 P_X, P_X2, P_R16, P_OL0, P_P2) = range(25)
NA, RG, BQ, S0, S1, EE, EL, SL0, SL1, FG = 2, "vava", "vava", "av", "av", "vava", "vava", "av", "av", "avav"
FE, FL = "aaaa", "vava"


def rank_program(g, core, T, topo):
    rank = T.rank_of(core)
    if rank is None:
        return
    N = len(T.cores)
    Q = {"v": g.vector, "a": g.scalar, "p": g.tensor, "g": g, "s": g.sync}
    SEM = {"v": "nv", "a": "na", "p": "np_", "g": "ng"}
    count = {k: 0 for k in SEM}
    known = {k: {} for k in Q}
    hist = {}
    total = {}

    def v(name, c0, c1, st=1, p0=0, p1=128):
        return (name if name in SCRATCH else "b_" + name, c0, c1, st, p0, p1)

    def ap(w):
        return T[w[0]][w[4]:w[5], w[1]:w[2]:w[3]] if w[3] != 1 else T[w[0]][w[4]:w[5], w[1]:w[2]]

    def foot(w):
        cols = 0
        for c in range(w[1], w[2], w[3]):
            cols |= 1 << c
        banks = 0
        if w[0] in ("pa", "pb"):
            for k in range(w[1] // 512, (w[2] - 1) // 512 + 1):
                banks |= 1 << k
        return cols, ((1 << w[5]) - 1) ^ ((1 << w[4]) - 1), banks

    def wait(q, sem, n, more=None):
        if known[q].get(sem, 0) < n:
            Q[q].wait_ge(T.sem[sem], n)
            known[q][sem] = n
        for s2, n2 in (more or {}).items():
            if known[q].get(s2, 0) < n2:
                known[q][s2] = n2

    def op(q, fn, reads, writes, dma=None, after=(), chain=False):
        need = {}
        acc = [(w, False) for w in reads] + [(w, True) for w in writes]
        feet = [(w[0], wr) + foot(w) for w, wr in acc]
        for name, wr, cols, parts, banks in feet:
            for q2, sem, n, wr2, cols2, parts2, banks2, kn in hist.get(name, ()):
                hit = (wr or wr2) and (cols & cols2) and (parts & parts2)
                if q2 != q and (banks & banks2):
                    hit = True
                if chain and q2 == q and banks2:
                    hit = False
                if hit and need.get(sem, (0, None))[0] < n:
                    need[sem] = (n, kn)
        for sem, n in after:
            wait(q, sem, n)
        todo = sorted(need.items(), key=lambda e: -len(e[1][1]))
        for sem, (n, kn) in todo:
            wait(q, sem, n, kn)
        ins = fn()
        if dma == "remote":
            return
        if dma:
            ins.then_inc(T.sem[dma], 16)
            sem, n = dma, 16
        else:
            count[q] += 1
            sem, n = SEM[q], count[q]
            ins.then_inc(T.sem[sem], 1)
        total[sem] = n
        kn = dict(known[q])
        for name, wr, cols, parts, banks in feet:
            hist.setdefault(name, []).append((q if not dma else dma, sem, n, wr, cols, parts, banks, kn))

    def sc(x):
        return ap(x) if isinstance(x, tuple) else x

    def tl(*xs):
        return [x for x in xs if isinstance(x, tuple)]

    def src(w, off):
        return ap(w) if off is None else ap(w).indirect(ap(off))

    def copy(q, out, in_, off=None, after=()):
        if q == "v":
            op(q, lambda: g.vector.tensor_copy(ap(out), src(in_, off)), tl(in_, off), [out], after=after)
        else:
            op(q, lambda: g.scalar.activation(ap(out), src(in_, off), ACT.Copy), tl(in_, off), [out], after=after)

    def scatter(win, off, in_):
        op("v", lambda: g.vector.tensor_copy(ap(win).indirect(ap(off)), ap(in_)), [in_, off], [win])

    def ts(out, in_, s1, op0, s2=None, op1=None, off=None):
        if op1 is None:
            op("v", lambda: g.vector.tensor_scalar(ap(out), src(in_, off), sc(s1), None, op0), tl(in_, off, s1), [out])
        else:
            op("v", lambda: g.vector.tensor_scalar(ap(out), src(in_, off), sc(s1), sc(s2), op0, op1),
               tl(in_, off, s1, s2), [out])

    def tt(out, a, b, o, off=None):
        op("v", lambda: g.vector.tensor_tensor(ap(out), src(a, off), ap(b), o), tl(a, b, off), [out])

    def act(out, in_, f, bias=0.0, scale=1.0, acc=None, off=None):
        if acc is None:
            op("a", lambda: g.scalar.activation(ap(out), src(in_, off), f, bias=sc(bias), scale=sc(scale)),
               tl(in_, bias, scale, off), [out])
        else:
            op("a", lambda: g.scalar.activation(ap(out), ap(in_), f, accum_out=ap(acc)), [in_], [out, acc])

    def fill(w, c):
        op("v", lambda: g.vector.memset(ap(w), c), [], [w])

    def turn(out, in_):
        op("v", lambda: g.vector.transpose(ap(out), ap(in_)), [in_], [out])

    def iota(out, pat, base=0, cm=0):
        if SCRATCH[out[0]][2] == I32:
            op("g", lambda: g.iota(ap(out), pat, base, cm), [], [out])
        else:
            op("g", lambda: g.iota(ap(out), pat, base, cm, allow_small_or_imprecise_dtypes=True), [], [out])

    def quant(name, c0, tile, t0, n):
        o, s, i = v("q" + name, c0, c0 + n), v("s" + name, c0, c0 + n), v(tile, t0, t0 + 4 * n)
        op("v", lambda: g.vector.quantize_mx(ap(o), ap(s), ap(i)), [i], [o, s])

    def mm(ps, bank, a, a0, b, b0, n, start=True, stop=True, after=()):
        o = v(ps, 512 * bank, 512 * bank + n)
        w = [v("q" + a, a0, a0 + 128), v("s" + a, a0, a0 + 128), v("q" + b, b0, b0 + n), v("s" + b, b0, b0 + n)]
        op("p", lambda: g.tensor.matmul_mx(ap(o), ap(w[0]), ap(w[1]), ap(w[2]), ap(w[3]), start, stop), w, [o],
           after=after, chain=not start)

    def pick(dst, d0, n, win, w0, w1, off):
        o, i = v("q" + dst, d0, d0 + n), v("q" + win, w0, w1)
        op("v", lambda: g.vector.tensor_copy(ap(o).bitcast(dt.uint32), ap(i).bitcast(dt.uint32).indirect(ap(off))),
           [i, off], [o])
        copy("a", v("s" + dst, d0, d0 + n), v("s" + win, w0, w1), off)

    def dma(q, sem, out, in_, reads, writes, after=()):
        op(q, lambda: Q[q].dma_start(out, in_), reads, writes, dma=sem, after=after)

    sent = [0]

    def peer(t, sign):
        return T.cores[(rank + sign * (1 + t)) % N]

    def send(t, out, in_, sem):
        dst = peer(t, 1)
        rid, pid = topo.addr(dst)[:2]
        a, b = ap(out), ap(in_)
        if SCRATCH[out[0]][2] == QX:
            a, b = a.bitcast(dt.uint8), b.bitcast(dt.uint8)
        op("g", lambda: g.remote_dma(a, b, T.sem[sem], T.sem["sent"], pid, rid, topo.mask(core, dst)), [in_], [],
           dma="remote")
        sent[0] += len(topo.engines(core, dst))

    def send_codes(t, name, n, at):
        send(t, v("qg%d" % t, at, at + n), v("q" + name, 0, n), "ag%d" % t)
        send(t, v("sg%d" % t, at, at + n), v("s" + name, 0, n), "ag%d" % t)

    def lands(t, calls):
        return calls * len(topo.engines(peer(t, -1), core))

    def pc(k, p0=0, p1=128):
        return v("pc", k, k + 1, 1, p0, p1)

    def lu(a, n):
        return v("lu", a, a + n)

    ID = ACT.Identity

    def ranks(k, mid=None):
        turn(v("xtt", 0, 160), v("row", 16, 176))
        turn(v("xtt", 160, 352), v("row", 0, 192))
        if k == 0:
            quant("e", 384, "et", 0, 128)
            unpack("x", C)
        copy("v", v("col", 0, 16), v("xtt", 0, 352), lu(GL, 1))
        tt(v("db", 0, C), v("xtt", 0, 352), v("row", 16, 176), ALU.is_equal, off=lu(SB, 10))
        act(v("ncol", 0, 16), v("xtt", 0, 352), ACT.Copy, 0.0, -1.0, off=lu(GL, 1))
        for c in range(NA):
            act(v("cm", 176 * c + 16, 160 * c + 160), v("row", 32 + 16 * c, 176), ACT.Sign, v("ncol", c, c + 1))
        for c in range(9):
            ts(v("cm", 160 * c, 176 * c + 16), v("row", 16, 32 + 16 * c), v("col", c, c + 1), ALU.is_ge)
            if NA <= c:
                ts(v("cm", 176 * c + 16, 160 * c + 160), v("row", 32 + 16 * c, 176), v("col", c, c + 1), ALU.is_gt)
            act(v("cm", 160 * c, 160 * c + 160), v("cm", 160 * c, 160 * c + 160), ACT.Relu, acc=v("acc", c, c + 1))
        ts(v("cm", 1440, 1600), v("row", 16, 176), v("col", 9, 10), ALU.is_ge)
        op("v", lambda: g.vector.tensor_tensor_scan(ap(v("dc", 0, C)), ap(v("db", 0, C)), ap(v("rst", 0, C)), 0.0,
                                                    ALU.add, ALU.mult),
           [v("rst", 0, C), v("db", 0, C)], [v("dc", 0, C)])
        op("v", lambda: g.vector.tensor_reduce(ap(v("acc", 9, 10)), ap(v("cm", 1440, 1600)), AxisListType.X, ALU.add),
           [v("cm", 1440, 1600)], [v("acc", 9, 10)])
        if mid:
            mid()
        rk = v("rk%d" % (k % 2), 0, 10)
        tt(rk, v("acc", 0, 10), v("dc", 15, C, 16), ALU.subtract)
        ts(v("ru", 0, 10), rk, -1.0, ALU.add)

    def invert(k):
        scatter(v("inv", 16, 176), v("ru", 0, 10), v("ir" if k < 2 else "val%d" % (k % 2), 0, C))
        if k == 0:
            copy("v", lu(LA, PL + 32 - LA), v("lt", LA, PL + 32))
        if k == 1:
            quant("b", 0, "kl", 0, 128)
        n = C if k == 0 else KEEP
        turn(v("tt", 0, n), v("inv", 16, 16 + n))
        turn(v("tt", 160, 192 + n), v("inv", 0, 32 + n))
        copy("v", v("ls%d" % k, 0, 16), v("tt", 0, 352), lu(GL, 1))
        if k > 0:
            send(k - 1, v("ll%d" % (k - 1), 0, 4), v("ls%d" % k, 0, 4), "al%d" % (k - 1))

    def keep_rank(k):
        ts(v("rs", 0, 10), v("rk%d" % (k % 2), 0, 10), 2.0, ALU.mult, pc(P_P2), ALU.add)

    def keep_val(k):
        if 0 < k < R:
            copy("a", v("val%d" % ((k + 1) % 2), 0, C), v("ir", 0, C), v("ru", 0, 10))

    def regather(out, win, step, width, n, lst, qs):
        for t in range(4):
            copy(qs[t], v(out, t, 4 * n, 4), v(win, step * t, step * t + width), v(lst, 0, n // 16))

    def flat(at, n, qs):
        for b in range(4):
            copy(qs[b], v("sp", PL_W * b + at, PL_W * b + at + n), v("si", 4 * at + b, 4 * (at + n), 4))

    def unpack(name, n, after=()):
        for b in range(4):
            mm("pa", b, "e", 128 * b, name, 0, n, after=after)

    def evac(out, at, n, planar, qs):
        for b in range(4):
            o = v(out, C * b, C * b + n) if planar else v(out, 4 * at + b, 4 * (at + n), 4)
            copy(qs[b], o, v("pa", 512 * b, 512 * b + n))

    def theirs(t):
        unpack("g%d" % t, C, after=[("ag%d" % t, lands(t, 2 if t == 0 else 4))])
        evac("gp", 0, C, True, "aaaa")

    def ab_early():
        copy("a", v("abe", 384, 768), v("si", 0, 384), lu(LB, 24))
        quant("ab", 192, "si", 0, 128)
        copy("v", v("abe", 0, 384), v("si", 0, 384), lu(LA, 24))
        quant("ab", 0, "abe", 0, 192)

    def ab_late():
        copy("v", v("abl", 0, 256), v("si", 0, 640), lu(LA + 24, 16))
        copy("a", v("abl", 256, 512), v("si", 0, 640), lu(LB + 24, 16))
        quant("ab", 320, "abl", 0, 128)

    def trial(late, h):
        n, name, ps = (128, "yl", "pa") if late else (192, "ye", "pb")
        if late:
            pick(name, 2 * n * h, 2 * n, "ab", 192, 448, lu(PL + 16 * h, 16))
        else:
            pick(name, 2 * n * h, 2 * n, "ab", 0, 320, lu(PE + 24 * h, 24))
        for k in (2 * h, 2 * h + 1):
            mm(ps, k, "up", 0, name, n * k, n)

    def scores(late, h, qs):
        n, at, ps = (128, 192, "pa") if late else (192, 0, "pb")
        for k in (2 * h, 2 * h + 1):
            copy(qs[k % 2], v("xs", at, at + n, 1, 32 * k, 32 * k + 32), v(ps, 512 * k, 512 * k + n, 1, 32 * k, 32 * k + 32))

    def to_row():
        copy("v", v("row", 16, 112), v("xs", 0, 320), v("rs", 0, 6))
        copy("a", v("row", 112, 176), v("xs", 0, 320), v("rs", 6, 10))

    def take(t):
        for b in range(4):
            copy(BQ[b], v("bt", b, 256, 4), v("gp", C * b, C * b + C), v("ll%d" % t, 0, 4),
                 after=[("al%d" % t, lands(t, 1))])
        quant("b", 64, "bt", 0, 128)
        for b in range(4):
            mm("pa", b, "w", 128 * b, "b", 64, 128, True, False)
            mm("pa", b, "e", 128 * b, "b", 0, 128, False, True)

    def layer(last):
        for b in range(4):
            act(v("rl", 64 * b, 64 * b + 64), v("pa", 512 * b, 512 * b + 64), ACT.Relu, 0.0, 0.03125)
            tt(v("sp", PL_W * b + C, PL_W * (b + 1)) if last else v("kl", b, 256, 4),
               v("rl", 64 * b, 64 * b + 64), v("pa", 512 * b + 64, 512 * b + 128), ALU.add)

    dma("a", "du", ap(v("ut", 0, 512)), T.u[:], [], [v("ut", 0, 512)])
    dma("s", "dx", ap(v("xt", 0, 640)), T.x[:], [], [v("xt", 0, 640)])
    iota(v("pi", 0, 1), [[0, 1]], 0, 1)
    iota(v("up", 0, 8), [[16, 8]])
    iota(v("c40", 0, 40), [[1, 40]])
    iota(v("lt", PE, PE + 48), [[0, 4], [4, 12]])
    iota(v("lt", PL, PL + 32), [[0, 4], [4, 8]])
    fill(v("ones", 0, 516), 1.0)
    p_ = v("pi", 0, 1)
    AND, SHR = ALU.bitwise_and, ALU.logical_shift_right
    ts(v("pi", 1, 2), p_, 15, AND)
    ts(v("pi", 2, 3), p_, 4, SHR, 1, AND)
    ts(v("pi", 3, 4), p_, 1, AND)
    ts(v("pi", 4, 5), p_, 15, AND, 1, SHR)
    ts(v("pi", 5, 6), p_, 15, AND, 2, SHR)
    ts(v("pi", 6, 7), p_, 8, AND, 1, SHR)
    ts(v("pi", 7, 8), p_, 3, AND)
    copy("v", lu(UP, 8), v("up", 0, 8))
    copy("v", v("pc", 0, 7), v("pi", 1, 8))
    op("g", lambda: g.affine_select(ap(v("et", 0, 516)), ap(v("ones", 0, 516)), [[-1, 516]], ALU.is_equal, 0.0, 3, 4),
       [v("ones", 0, 516)], [v("et", 0, 516)])
    iota(v("q16", 0, C), [[0, 10], [1, 16]])
    iota(v("ir", 0, C), [[1, C]])
    act(pc(P_X), pc(P_PAR), ID, pc(P_R1), -1.0)
    act(pc(P_R16), pc(P_R), ID, 0.0, 16.0)
    act(pc(P_S0), pc(P_PAR), ID, 0.0, 176.0)
    act(pc(P_S1), pc(P_PAR), ID, 192.0, -176.0)
    act(pc(P_X2), pc(P_X), ACT.Square)
    act(v("lt", SB, SB + 10, 2), v("c40", 0, 5), ID, pc(P_S0), 32.0)
    act(v("lt", SB + 1, SB + 10, 2), v("c40", 0, 5), ID, pc(P_S1), 32.0)
    act(v("lt", GL, GL + 1), pc(P_X2), ID, pc(P_R16), 176.0)
    for o, i, scale, bias in (
            (P_W, P_T1, 1.0, pc(P_T2)), (P_IP, P_PAR, -1.0, 1.0), (P_MA, P_PAR, -8.0, 16.0), (P_MB, P_PAR, 8.0, 8.0),
            (P_D, P_R, -1.0, pc(P_W)), (P_OE, P_R1, 96.0, pc(P_RH)), (P_OL0, P_R1, 64.0, pc(P_RH)),
            (P_HE, P_RQ, 1.0, 192.0), (P_HL, P_RQ, 1.0, 48.0), (P_A, P_PAR, pc(P_D), pc(P_R)),
            (P_B, P_IP, pc(P_D), pc(P_R)), (P_OL, P_OL0, 1.0, 128.0), (P_P2, P_PAR, 1.0, -2.0)):
        ts(pc(o), pc(i), scale, ALU.mult, bias, ALU.add)
    fill(v("row", 0, 16), 0.0)
    fill(v("row", 176, 192), 0.0)
    fill(v("inv", 0, 192), 0.0)
    ts(lu(GL, 1), v("lt", GL, GL + 1), 351.0, ALU.min)
    copy("v", lu(SB, 10), v("lt", SB, SB + 10))
    act(v("lt", PE, PE + 48), v("lt", PE, PE + 48), ID, pc(P_HE))
    act(v("lt", PL, PL + 32), v("lt", PL, PL + 32), ID, pc(P_HL))
    act(v("lt", LA, LA + 40), v("c40", 0, 40), ID, pc(P_A), pc(P_MA))
    act(v("lt", LB, LB + 40), v("c40", 0, 40), ID, pc(P_B), pc(P_MB))

    def own_lists(k):
        a, z = 32 * k, 32 * k + 32
        act(v("lt", PE + 12 * k, PE + 12 * k + 12, 1, a, z), v("c40", 0, 12, 1, a, z), ID, pc(P_OE, a, z), 8.0)
        act(v("lt", PL + 8 * k, PL + 8 * k + 8, 1, a, z), v("c40", 0, 8, 1, a, z), ID, pc(P_OL, a, z), 8.0)
    own_lists(0)
    own_lists(1)
    quant("u", 0, "ut", 0, 128)
    pick("up", 0, 128, "u", 0, 128, lu(UP, 8))
    quant("x", 0, "xt", 0, C)
    mm("pb", 0, "up", 0, "x", 0, C)
    send_codes(0, "x", C, 0)
    iota(v("kl", 0, 512), [[0, 512]])
    iota(v("ke", 384, 512), [[0, 128]])
    iota(v("bt", 256, 512), [[0, 256]])
    dma("s", "dwc", ap(v("qw", 0, 512)).bitcast(dt.uint8), T.wc[:], [], [v("qw", 0, 512)], after=[("dx", 16), ("du", 16)])
    dma("s", "dws", ap(v("sw", 0, 512)), T.ws[:], [], [v("sw", 0, 512)])
    dma("s", "dv", ap(v("vt", 0, 512)), T.v[:], [], [v("vt", 0, 512)])
    own_lists(2)
    own_lists(3)
    quant("e", 0, "et", 3, 128)
    quant("e", 128, "et", 2, 128)
    quant("e", 256, "et", 1, 128)
    copy("a", v("row", 16, 176), v("pb", 0, C))
    ts(v("rst", 0, C), v("q16", 0, C), pc(P_R), ALU.is_gt)

    ranks(0, lambda: evac("t0", 0, C, True, "aaaa"))
    invert(0)
    regather("si", "t0", C, C, C, "ls0", "vava")
    ab_early()
    keep_rank(0)
    trial(False, 0)
    ab_late()
    trial(False, 1)
    scores(False, 0, "av")
    trial(True, 0)
    scores(False, 1, "av")
    trial(True, 1)
    scores(True, 0, "av")
    scores(True, 1, "av")
    to_row()

    for t in range(R):
        k = t + 1
        ranks(k, lambda: theirs(t))
        keep_val(k)
        invert(k)
        if k == R:
            break
        regather("ke", "sp" if t else "t0", PL_W if t else C, C, KEEP, "ls%d" % k, RG)
        quant("se%d" % k, 0, "ke", 0, 128)
        unpack("se%d" % k, 128)
        send_codes(k, "se%d" % k, KEEP, 0)
        keep_rank(k)
        evac("si", 0, KEEP, False, EE)
        ab_early()
        flat(0, KEEP, FE)
        take(t)
        trial(False, 0)
        layer(False)
        quant("sl%d" % k, 0, "kl", 0, 128)
        unpack("sl%d" % k, 128)
        send_codes(k, "sl%d" % k, M, KEEP)
        trial(False, 1)
        evac("si", KEEP, M, False, EL)
        scores(False, 0, S0)
        ab_late()
        scores(False, 1, S1)
        trial(True, 0)
        trial(True, 1)
        scores(True, 0, SL0)
        scores(True, 1, SL1)
        to_row()
        flat(KEEP, M, FL)

    new, old = v("rk%d" % (R % 2), 0, 10), v("rk%d" % ((R - 1) % 2), 0, 10)
    f1, f2, f3, f4 = (v("f%d" % i, 0, 10) for i in (1, 2, 3, 4))
    tt(f1, new, old, ALU.subtract)
    ts(f2, new, float(KEEP), ALU.is_gt)
    scatter(v("olr", 0, C), v("ru", 0, 10), v("ir", 0, C))
    ts(f3, f1, float(C - KEEP), ALU.add)
    quant("v", 0, "vt", 0, 128)
    tt(f1, f3, f2, ALU.mult)
    dma("s", "dol", T.ol[:], T["b_olr"][0:128:16, 0:C], [v("olr", 0, C)], [])
    tt(f4, f1, old, ALU.add)
    ts(v("fl", 0, 10), f4, -1.0, ALU.add)
    take(R - 1)
    layer(True)
    regather("tf", "sp", PL_W, PL_W, C, "fl", FG)
    quant("f", 0, "tf", 0, C)
    mm("pb", 0, "v", 0, "f", 0, C)
    dma("s", "doc", T.oc[:], ap(v("qf", 0, C)).bitcast(dt.uint8), [v("qf", 0, C)], [])
    for k in range(4):
        w = v("sf", 0, C, 1, 32 * k, 32 * k + 4)
        dma("sa"[k % 2], "ds%d" % k, T.osc[4 * k:4 * k + 4, 0:C], ap(w), [w], [])
    copy("v", v("yo", 0, C), v("pb", 0, C))
    dma("a", "dy", T.y[:], ap(v("yo", 0, C)), [v("yo", 0, C)], [])

    wait("g", "sent", sent[0])
    for sem, n in total.items():
        if max(known[q].get(sem, 0) for q in Q) < n or sem in SEM.values():
            wait("s", sem, n)
